import numpy as np
import ml_dtypes


def mxq(x, axis, fmt="e4m3"):
    dtype, down = {"e4m3": (ml_dtypes.float8_e4m3fn, 7), "e5m2": (ml_dtypes.float8_e5m2, 14)}[fmt]
    v = np.moveaxis(np.asarray(x, np.float32).astype(ml_dtypes.bfloat16).astype(np.float64), axis, -1)
    blocks = v.reshape(v.shape[:-1] + (-1, 32))
    amax = np.abs(blocks).max(-1, keepdims=True)
    byte = np.maximum(np.where(amax > 0, np.frexp(amax)[1] - 1 + 127, 0) - down, 1)
    scale = np.exp2(byte - 127.0)
    codes = (blocks / scale).astype(np.float32).astype(dtype).astype(np.float64)
    return np.moveaxis((codes * scale).reshape(v.shape), -1, axis)


WIDE = False


def mx_kscale(k):
    if not WIDE:
        return np.ones(k)
    levels = np.array([10, -10, 5, -5, 0])
    if k % 512:
        return np.exp2(np.random.permutation(np.resize(levels, k // 32))).repeat(32)
    a = np.empty((k // 512, 16))
    for p in range(k // 512):
        a[p, :8] = np.random.permutation(np.resize(levels, 8))
        for g in range(8):
            far = levels[np.abs(levels - a[p, g]) >= 10]
            a[p, g + 8] = far[np.random.randint(len(far))]
    return np.exp2(a.ravel()).repeat(32)


def f64(x):
    return np.asarray(x).astype(np.float64)


def striped8(idx):
    return np.concatenate([x.reshape(-1, 16).T for x in idx]).astype(np.uint16)


def runs(offs, k):
    lists = np.stack([offs[16 * r : 16 * r + 16].T.reshape(-1) for r in range(8)]).astype(np.int64)
    return lists[np.arange(k) % 512 // 64]


def pack_weight(w):
    k, n = w.shape
    w = f64(np.asarray(w, np.float32).astype(ml_dtypes.bfloat16)).reshape(k // 32, 32, n)
    amax = np.abs(w).max(1)
    byte = np.clip(np.where(amax > 0, np.frexp(amax)[1] - 1 + 127 - 7, 1), 1, 254)
    scaled = (w * np.exp2(127.0 - byte)[:, None, :]).reshape(k, n).astype(np.float32)
    words = np.ascontiguousarray(scaled.reshape(k // 512, 128, 4, n).transpose(0, 1, 3, 2)).astype(ml_dtypes.float8_e4m3fn).view(np.uint8)
    return words, np.ascontiguousarray(byte.astype(np.uint8).reshape(k // 512, 16, n))


def unpack_weight(words, scales):
    g, p, n, _ = words.shape
    vals = np.ascontiguousarray(words).view(ml_dtypes.float8_e4m3fn).astype(np.float64) * np.repeat(np.exp2(scales.astype(np.float64) - 127.0), 8, axis=1)[..., None]
    return vals.transpose(0, 1, 3, 2).reshape(g * 512, n)


K, T, S, N, G, H, W = 512, 2048, 512, 512, 2048, 512, 256


def setup_inputs():
    n = np.random.standard_normal
    s = mx_kscale(K)[:, None]
    u = mx_kscale(S)
    packed_xT = pack_weight(n((K, T)) * s)
    packed_dT = pack_weight(n((K, G)) / s)
    perm = np.stack([np.random.permutation(S) for _ in range(8)])
    return {
        "x_words": packed_xT[0],
        "x_scales": packed_xT[1],
        "d_words": packed_dT[0],
        "d_scales": packed_dT[1],
        "gn": (np.random.uniform(0.5, 1.5, (H, 1)) * u[:, None]).astype(np.float32),
        "w1": (n((H, N)) / np.sqrt(H) / u[:, None]).astype(np.float32),
        "offs": striped8(np.random.randint(0, T, (8, S))),
        "k1": striped8(np.random.randint(0, G, (8, H))),
        "n1": striped8(perm[:, :W]),
        "n2": striped8(perm[:, W:]),
        "n3": striped8(np.stack([np.random.permutation(S) for _ in range(8)])),
    }


def reference(x_words, x_scales, d_words, d_scales, gn, w1, offs, k1, n1, n2, n3):
    d_k1 = unpack_weight(d_words, d_scales)[np.arange(K)[:, None], runs(k1, K)]
    xq = unpack_weight(x_words, x_scales)[np.arange(K)[:, None], runs(offs, K)]
    h = 0.0625 * (d_k1.T @ xq)
    z = f64(gn) * h
    h2 = mxq(f64(w1), 0, "e4m3").T @ mxq(z, 0, "e4m3")
    pa = h2[np.arange(N)[:, None], runs(n1, N)]
    pb = h2[np.arange(N)[:, None], runs(n2, N)]
    rb = pa - pb
    ra = pa + pb
    ds = np.zeros((N, S))
    ds[np.arange(N)[:, None], runs(n1, N)] = ra
    dt = ds.copy()
    dt[np.arange(N)[:, None], runs(n2, N)] = rb
    return np.maximum(dt, dt[np.arange(N)[:, None], runs(n3, N)])

@@ -1,0 +1,219 @@
+from contextlib import ExitStack
+
+import concourse.mybir as mybir
+
+K, T, S, H, N, W = 512, 2048, 512, 512, 512, 256
+FLOPS = 2 * K * H * S + 2 * H * N * S
+
+F32 = mybir.dt.float32
+BF16 = mybir.dt.bfloat16
+I32 = mybir.dt.int32
+U32 = mybir.dt.uint32
+U16 = mybir.dt.uint16
+U8 = mybir.dt.uint8
+FP8X4 = mybir.dt.float8_e4m3fn_x4
+ALU = mybir.AluOpType
+COPY = mybir.ActivationFunctionType.Copy
+
+P = 128
+PACK = 4
+CHUNK = 128
+HALF = 256
+
+
+def tile_picked_hpqihaarh_none_p_kernel(
+    tc, x_words, x_scales, d_words, d_scales, gn, w1, offs, k1, n1, n2, n3, out
+):
+    nc = tc.nc
+    with ExitStack() as ctx:
+        keep = ctx.enter_context(tc.tile_pool(name="keep", bufs=1))
+        psum = ctx.enter_context(tc.psum_pool(name="psum", bufs=1))
+
+        def load_list(name, lists):
+            tile = keep.tile(list(lists.shape), U16, name=name)
+            nc.sync.dma_start(tile[:], lists)
+            return tile
+
+        def load_scales(name, scales):
+            tile = keep.tile([P, T], U8, name=name, align_bytes=64)
+            nc.sync.dma_start(
+                tile[:].bitcast(I32), scales[0].bitcast(I32).unsqueeze(1).to_broadcast([16, 8, T // 4])
+            )
+            return tile
+
+        def load_words(name, words):
+            tile = keep.tile([P, T], U32, name=name, align_bytes=64)
+            nc.sync.dma_start(tile[:].bitcast(I32), words[0].rearrange("p n t -> p (n t)").bitcast(I32))
+            return tile
+
+        k1_list = load_list("k1_list", k1)
+        d_scale_table = load_scales("d_scale_table", d_scales)
+        offs_list = load_list("offs_list", offs)
+        x_scale_table = load_scales("x_scale_table", x_scales)
+        gain = keep.tile([P, PACK], F32, name="gain")
+        nc.scalar.dma_start(gain[:], gn.rearrange("(p t) o -> p (t o)", t=PACK))
+        d_word_table = load_words("d_word_table", d_words)
+        x_word_table = load_words("x_word_table", x_words)
+        n1_list = load_list("n1_list", n1)
+        n2_list = load_list("n2_list", n2)
+        n3_list = load_list("n3_list", n3)
+
+        gain16 = keep.tile([P, PACK], F32, name="gain16")
+        nc.scalar.activation(gain16[:], gain[:], COPY, scale=0.0625)
+
+        d_scale_picked = keep.tile([P, H], U8, name="d_scale_picked", tag="stage0", align_bytes=64)
+        x_scale_picked = keep.tile([P, S], U8, name="x_scale_picked", tag="stage1", align_bytes=64)
+        planes = keep.tile([P, H + S], U8, name="planes", align_bytes=64)
+        nc.vector.tensor_copy(d_scale_picked[:], d_scale_table[:].indirect(k1_list[:]))
+        nc.vector.tensor_copy(x_scale_picked[:], x_scale_table[:].indirect(offs_list[:]))
+        nc.vector.tensor_copy(
+            planes[:, 0:H].rearrange("p (t a b) -> p a t b", t=PACK, b=16),
+            d_scale_picked[:].rearrange("p (a b t) -> p a t b", t=PACK, b=16),
+        )
+        nc.vector.tensor_copy(planes[:, H : H + S].bitcast(I32), x_scale_picked[:].bitcast(I32))
+        for a in range(1, 4):
+            nc.sync.dma_start(planes[a:P:32, :].bitcast(I32), planes[8 * a : P : 32, :].bitcast(I32))
+        w_rows = w1.rearrange("(p j) c -> p j c", j=PACK)
+        w_raw = []
+        for c in range(2):
+            piece = keep.tile([P, PACK, HALF], F32, name=f"w_raw{c}", tag=f"stage{c}", align_bytes=64)
+            nc.sync.dma_start(piece[:], w_rows[:, :, c * HALF : (c + 1) * HALF])
+            w_raw.append(piece)
+
+        d_picked = keep.tile([P, H], U32, name="d_picked", align_bytes=64)
+        d_dealt = keep.tile([P, H], U32, name="d_dealt", align_bytes=64)
+        nc.vector.tensor_copy(d_picked[:], d_word_table[:].indirect(k1_list[:]))
+        x_picked = [keep.tile([P, HALF], U32, name=f"x_picked{c}", align_bytes=64) for c in range(2)]
+        nc.vector.tensor_copy(
+            d_dealt[:].rearrange("p (t a b) -> p a t b", t=PACK, b=4),
+            d_picked[:].rearrange("p (a b t) -> p a t b", t=PACK, b=4),
+        )
+        nc.vector.tensor_copy(x_picked[0][:], x_word_table[:].indirect(offs_list[:, 0:16]))
+        nc.vector.tensor_copy(x_picked[1][:], x_word_table[:].indirect(offs_list[:, 16:32]))
+
+        w_bf = keep.tile([P, PACK, P, PACK], BF16, name="w_bf", align_bytes=64)
+        for c in range(2):
+            nc.scalar.copy(
+                w_bf[:, :, c * 64 : (c + 1) * 64, :].rearrange("p t m j -> p m t j"),
+                w_raw[c][:].rearrange("p j (m t) -> p m t j", t=PACK),
+            )
+        w_codes = keep.tile([P, N], U32, name="w_codes", align_bytes=64)
+        w_scale = keep.tile([P, N], U8, name="w_scale", align_bytes=64)
+
+        def quantize_w(t):
+            cols = slice(t * P, (t + 1) * P)
+            nc.vector.quantize_mx(
+                w_codes[:, cols].bitcast(FP8X4), w_scale[:, cols], w_bf[:, t].rearrange("p m j -> p (m j)")
+            )
+
+        z_codes = keep.tile([P, S], U32, name="z_codes", align_bytes=64)
+        z_scale = keep.tile([P, S], U8, name="z_scale", align_bytes=64)
+        z_bf = []
+
+        def first_product(c):
+            bank = psum.tile([P, PACK, CHUNK], F32, name=f"h{c}", tag=f"bank{c}")
+            xs = x_picked[c // 2][:, (c % 2) * CHUNK : (c % 2 + 1) * CHUNK]
+            for t in range(PACK):
+                nc.tensor.matmul_mx(
+                    bank[:, t, :],
+                    lhsT=d_dealt[:, t * P : (t + 1) * P].bitcast(FP8X4),
+                    lhsT_scale=planes[:, t * P : (t + 1) * P],
+                    rhs=xs.bitcast(FP8X4),
+                    rhs_scale=planes[:, H + c * CHUNK : H + (c + 1) * CHUNK],
+                    start=True,
+                    stop=True,
+                )
+            z = keep.tile([P, CHUNK, PACK], BF16, name=f"z_bf{c}", align_bytes=64)
+            nc.vector.tensor_tensor(
+                z[:],
+                bank[:].rearrange("p t n -> p n t"),
+                gain16[:].unsqueeze(1).to_broadcast([P, CHUNK, PACK]),
+                ALU.mult,
+            )
+            z_bf.append(z)
+
+        def quantize_z(c):
+            cols = slice(c * CHUNK, (c + 1) * CHUNK)
+            nc.vector.quantize_mx(
+                z_codes[:, cols].bitcast(FP8X4), z_scale[:, cols], z_bf[c][:].rearrange("p n t -> p (n t)")
+            )
+
+        first_product(0)
+        for c in range(1, 4):
+            first_product(c)
+            quantize_z(c - 1)
+        quantize_w(0)
+        quantize_z(3)
+        for t in range(1, 4):
+            quantize_w(t)
+
+        def second_product(dst, t, cols):
+            nc.tensor.matmul_mx(
+                dst,
+                lhsT=w_codes[:, t * P : (t + 1) * P].bitcast(FP8X4),
+                lhsT_scale=w_scale[:, t * P : (t + 1) * P],
+                rhs=z_codes[:, cols].bitcast(FP8X4),
+                rhs_scale=z_scale[:, cols],
+                start=True,
+                stop=True,
+            )
+
+        out_rows = out.rearrange("(p t) j -> p t j", t=PACK)
+        h2, pa, pb, npb, dt = {}, {}, {}, {}, {}
+
+        def results(t):
+            h2[t] = keep.tile([P, S], F32, name=f"h2_{t}", tag=f"row{t}")
+            if t == 0:
+                early = psum.tile([P, S - CHUNK], F32, name="h2_early", tag="bank4")
+                late = psum.tile([P, CHUNK], F32, name="h2_late", tag="bank5")
+                second_product(early[:, 0:HALF], t, slice(0, HALF))
+                second_product(early[:, HALF : S - CHUNK], t, slice(HALF, S - CHUNK))
+                second_product(late[:], t, slice(S - CHUNK, S))
+                nc.scalar.copy(h2[t][:, 0 : S - CHUNK], early[:])
+                nc.vector.tensor_copy(h2[t][:, S - CHUNK : S], late[:])
+            else:
+                bank = psum.tile([P, S], F32, name=f"h2_bank{t}", tag=f"bank{(5 + t) % 8}")
+                second_product(bank[:], t, slice(0, S))
+                nc.scalar.copy(h2[t][:], bank[:])
+            pa[t] = keep.tile([P, W], F32, name=f"pa{t}")
+            pb[t] = keep.tile([P, W], F32, name=f"pb{t}")
+            npb[t] = keep.tile([P, W], F32, name=f"npb{t}")
+            nc.scalar.activation(pa[t][:], h2[t][:].indirect(n1_list[:]), COPY)
+            if t == 0:
+                nc.vector.tensor_copy(pb[t][:], h2[t][:].indirect(n2_list[:]))
+            else:
+                nc.scalar.activation(pb[t][:], h2[t][:].indirect(n2_list[:]), COPY)
+            nc.scalar.activation(npb[t][:], pb[t][:], COPY, scale=-1.0)
+
+        def scatter_sums(t):
+            dt[t] = keep.tile([P, S], F32, name=f"dt{t}")
+            nc.vector.tensor_tensor(dt[t][:].indirect(n1_list[:]), pa[t][:], pb[t][:], ALU.add)
+
+        def scatter_differences(t):
+            nc.vector.tensor_tensor(dt[t][:].indirect(n2_list[:]), pa[t][:], npb[t][:], ALU.add)
+
+        def larger(t):
+            partner = keep.tile([P, S], F32, name=f"partner{t}", tag=f"row{(t + 1) % PACK}")
+            result = keep.tile([P, S], F32, name=f"result{t}")
+            last = t == PACK - 1
+            halves = [slice(c * HALF, (c + 1) * HALF) for c in range(2)]
+            nc.scalar.activation(partner[:, halves[0]], dt[t][:].indirect(n3_list[:, 0:16]), COPY)
+            if last:
+                nc.vector.tensor_copy(partner[:, halves[1]], dt[t][:].indirect(n3_list[:, 16:32]))
+                for cols in reversed(halves):
+                    nc.vector.tensor_tensor(result[:, cols], dt[t][:, cols], partner[:, cols], ALU.max)
+                    nc.sync.dma_start(out_rows[:, t, cols], result[:, cols])
+            else:
+                nc.scalar.activation(partner[:, halves[1]], dt[t][:].indirect(n3_list[:, 16:32]), COPY)
+                nc.vector.tensor_tensor(result[:], dt[t][:], partner[:], ALU.max)
+                nc.sync.dma_start(out_rows[:, t, :], result[:])
+
+        results(0)
+        scatter_sums(0)
+        scatter_differences(0)
+        for t in range(1, PACK):
+            results(t)
+            scatter_sums(t)
+            larger(t - 1)
+            scatter_differences(t)
+        larger(PACK - 1)

@@ -34,11 +34,10 @@ def tile_picked_hpqihaarh_none_p_kernel(
             nc.sync.dma_start(tile[:], lists)
             return tile
 
-        def load_scales(name, scales):
+        def load_scales(name, scales, engine):
             tile = keep.tile([P, T], U8, name=name, align_bytes=64)
-            nc.sync.dma_start(
-                tile[:].bitcast(I32), scales[0].bitcast(I32).unsqueeze(1).to_broadcast([16, 8, T // 4])
-            )
+            engine.memset(tile[:].bitcast(I32), 0)
+            nc.sync.dma_start(tile[0:P:8, :].bitcast(I32), scales[0].bitcast(I32))
             return tile
 
         def load_words(name, words):
@@ -46,23 +45,23 @@ def tile_picked_hpqihaarh_none_p_kernel(
             nc.sync.dma_start(tile[:].bitcast(I32), words[0].rearrange("p n t -> p (n t)").bitcast(I32))
             return tile
 
+        d_scale_table = load_scales("d_scale_table", d_scales, nc.gpsimd)
+        x_scale_table = load_scales("x_scale_table", x_scales, nc.vector)
         k1_list = load_list("k1_list", k1)
-        d_scale_table = load_scales("d_scale_table", d_scales)
         offs_list = load_list("offs_list", offs)
-        x_scale_table = load_scales("x_scale_table", x_scales)
-        gain = keep.tile([P, PACK], F32, name="gain")
-        nc.scalar.dma_start(gain[:], gn.rearrange("(p t) o -> p (t o)", t=PACK))
-        d_word_table = load_words("d_word_table", d_words)
-        x_word_table = load_words("x_word_table", x_words)
         n1_list = load_list("n1_list", n1)
         n2_list = load_list("n2_list", n2)
         n3_list = load_list("n3_list", n3)
+        d_word_table = load_words("d_word_table", d_words)
+        gain = keep.tile([P, PACK], F32, name="gain")
+        nc.sync.dma_start(gain[:], gn.rearrange("(p t) o -> p (t o)", t=PACK))
+        x_word_table = load_words("x_word_table", x_words)
 
         gain16 = keep.tile([P, PACK], F32, name="gain16")
         nc.scalar.activation(gain16[:], gain[:], COPY, scale=0.0625)
 
-        d_scale_picked = keep.tile([P, H], U8, name="d_scale_picked", tag="stage0", align_bytes=64)
-        x_scale_picked = keep.tile([P, S], U8, name="x_scale_picked", tag="stage1", align_bytes=64)
+        d_scale_picked = keep.tile([P, H], U8, name="d_scale_picked", align_bytes=64)
+        x_scale_picked = keep.tile([P, S], U8, name="x_scale_picked", tag="stage", align_bytes=64)
         planes = keep.tile([P, H + S], U8, name="planes", align_bytes=64)
         nc.vector.tensor_copy(d_scale_picked[:], d_scale_table[:].indirect(k1_list[:]))
         nc.vector.tensor_copy(x_scale_picked[:], x_scale_table[:].indirect(offs_list[:]))
@@ -74,10 +73,11 @@ def tile_picked_hpqihaarh_none_p_kernel(
         for a in range(1, 4):
             nc.sync.dma_start(planes[a:P:32, :].bitcast(I32), planes[8 * a : P : 32, :].bitcast(I32))
         w_rows = w1.rearrange("(p j) c -> p j c", j=PACK)
+        w_tile = keep.tile([P, PACK * N], F32, name="w_tile", tag="stage", align_bytes=64)
         w_raw = []
         for c in range(2):
-            piece = keep.tile([P, PACK, HALF], F32, name=f"w_raw{c}", tag=f"stage{c}", align_bytes=64)
-            nc.sync.dma_start(piece[:], w_rows[:, :, c * HALF : (c + 1) * HALF])
+            piece = w_tile[:, c * PACK * HALF : (c + 1) * PACK * HALF].rearrange("p (j c) -> p j c", j=PACK)
+            nc.sync.dma_start(piece, w_rows[:, :, c * HALF : (c + 1) * HALF])
             w_raw.append(piece)
 
         d_picked = keep.tile([P, H], U32, name="d_picked", align_bytes=64)
@@ -92,18 +92,19 @@ def tile_picked_hpqihaarh_none_p_kernel(
         nc.vector.tensor_copy(x_picked[1][:], x_word_table[:].indirect(offs_list[:, 16:32]))
 
         w_bf = keep.tile([P, PACK, P, PACK], BF16, name="w_bf", align_bytes=64)
-        for c in range(2):
-            nc.scalar.copy(
-                w_bf[:, :, c * 64 : (c + 1) * 64, :].rearrange("p t m j -> p m t j"),
-                w_raw[c][:].rearrange("p j (m t) -> p m t j", t=PACK),
-            )
+        for t in range(PACK):
+            for c in range(2):
+                nc.scalar.copy(
+                    w_bf[:, t, c * 64 : (c + 1) * 64, :].rearrange("p (a i) j -> p a i j", i=4),
+                    w_raw[c].rearrange("p j (a t i) -> p t a i j", t=PACK, i=4)[:, t],
+                )
         w_codes = keep.tile([P, N], U32, name="w_codes", align_bytes=64)
         w_scale = keep.tile([P, N], U8, name="w_scale", align_bytes=64)
 
-        def quantize_w(t):
-            cols = slice(t * P, (t + 1) * P)
+        def quantize_w(t0, t1):
+            cols = slice(t0 * P, t1 * P)
             nc.vector.quantize_mx(
-                w_codes[:, cols].bitcast(FP8X4), w_scale[:, cols], w_bf[:, t].rearrange("p m j -> p (m j)")
+                w_codes[:, cols].bitcast(FP8X4), w_scale[:, cols], w_bf[:, t0:t1].rearrange("p t m j -> p (t m j)")
             )
 
         z_codes = keep.tile([P, S], U32, name="z_codes", align_bytes=64)
@@ -142,10 +143,9 @@ def tile_picked_hpqihaarh_none_p_kernel(
         for c in range(1, 4):
             first_product(c)
             quantize_z(c - 1)
-        quantize_w(0)
+        quantize_w(0, 1)
         quantize_z(3)
-        for t in range(1, 4):
-            quantize_w(t)
+        quantize_w(1, PACK)
 
         def second_product(dst, t, cols):
             nc.tensor.matmul_mx(
@@ -158,7 +158,7 @@ def tile_picked_hpqihaarh_none_p_kernel(
                 stop=True,
             )
 
-        out_rows = out.rearrange("(p t) j -> p t j", t=PACK)
+        out_rows = out.rearrange("(a t i) j -> t a i j", t=PACK, i=4)
         h2, pa, pb, npb, dt = {}, {}, {}, {}, {}
 
         def results(t):
@@ -202,11 +202,11 @@ def tile_picked_hpqihaarh_none_p_kernel(
                 nc.vector.tensor_copy(partner[:, halves[1]], dt[t][:].indirect(n3_list[:, 16:32]))
                 for cols in reversed(halves):
                     nc.vector.tensor_tensor(result[:, cols], dt[t][:, cols], partner[:, cols], ALU.max)
-                    nc.sync.dma_start(out_rows[:, t, cols], result[:, cols])
+                    nc.sync.dma_start(out_rows[t][:, :, cols], result[:, cols])
             else:
                 nc.scalar.activation(partner[:, halves[1]], dt[t][:].indirect(n3_list[:, 16:32]), COPY)
                 nc.vector.tensor_tensor(result[:], dt[t][:], partner[:], ALU.max)
-                nc.sync.dma_start(out_rows[:, t, :], result[:])
+                nc.sync.dma_start(out_rows[t], result[:])
 
         results(0)
         scatter_sums(0)

@@ -17,8 +17,14 @@ COPY = mybir.ActivationFunctionType.Copy
 
 P = 128
 PACK = 4
-CHUNK = 128
-HALF = 256
+BLOCK_ROWS = 8
+QUADRANT = 32
+CHUNK = S // PACK
+HALF = S // 2
+HALF_LIST = HALF // 16
+LINE_WORDS = 4
+LINE_BYTES = 16
+LAG = 2
 
 
 def tile_picked_hpqihaarh_none_p_kernel(
@@ -34,10 +40,10 @@ def tile_picked_hpqihaarh_none_p_kernel(
             nc.sync.dma_start(tile[:], lists)
             return tile
 
-        def load_scales(name, scales, engine):
+        def load_scales(name, scales, clearing_engine):
             tile = keep.tile([P, T], U8, name=name, align_bytes=64)
-            engine.memset(tile[:].bitcast(I32), 0)
-            nc.sync.dma_start(tile[0:P:8, :].bitcast(I32), scales[0].bitcast(I32))
+            clearing_engine.memset(tile[:].bitcast(I32), 0)
+            nc.sync.dma_start(tile[0:P:BLOCK_ROWS, :].bitcast(I32), scales[0].bitcast(I32))
             return tile
 
         def load_words(name, words):
@@ -66,12 +72,15 @@ def tile_picked_hpqihaarh_none_p_kernel(
         nc.vector.tensor_copy(d_scale_picked[:], d_scale_table[:].indirect(k1_list[:]))
         nc.vector.tensor_copy(x_scale_picked[:], x_scale_table[:].indirect(offs_list[:]))
         nc.vector.tensor_copy(
-            planes[:, 0:H].rearrange("p (t a b) -> p a t b", t=PACK, b=16),
-            d_scale_picked[:].rearrange("p (a b t) -> p a t b", t=PACK, b=16),
+            planes[:, 0:H].rearrange("p (t a b) -> p a t b", t=PACK, b=LINE_BYTES),
+            d_scale_picked[:].rearrange("p (a b t) -> p a t b", t=PACK, b=LINE_BYTES),
         )
         nc.vector.tensor_copy(planes[:, H : H + S].bitcast(I32), x_scale_picked[:].bitcast(I32))
-        for a in range(1, 4):
-            nc.sync.dma_start(planes[a:P:32, :].bitcast(I32), planes[8 * a : P : 32, :].bitcast(I32))
+        for a in range(1, PACK):
+            nc.sync.dma_start(
+                planes[a:P:QUADRANT, :].bitcast(I32), planes[BLOCK_ROWS * a : P : QUADRANT, :].bitcast(I32)
+            )
+
         w_rows = w1.rearrange("(p j) c -> p j c", j=PACK)
         w_tile = keep.tile([P, PACK * N], F32, name="w_tile", tag="stage", align_bytes=64)
         w_raw = []
@@ -85,18 +94,19 @@ def tile_picked_hpqihaarh_none_p_kernel(
         nc.vector.tensor_copy(d_picked[:], d_word_table[:].indirect(k1_list[:]))
         x_picked = [keep.tile([P, HALF], U32, name=f"x_picked{c}", align_bytes=64) for c in range(2)]
         nc.vector.tensor_copy(
-            d_dealt[:].rearrange("p (t a b) -> p a t b", t=PACK, b=4),
-            d_picked[:].rearrange("p (a b t) -> p a t b", t=PACK, b=4),
+            d_dealt[:].rearrange("p (t a b) -> p a t b", t=PACK, b=LINE_WORDS),
+            d_picked[:].rearrange("p (a b t) -> p a t b", t=PACK, b=LINE_WORDS),
         )
-        nc.vector.tensor_copy(x_picked[0][:], x_word_table[:].indirect(offs_list[:, 0:16]))
-        nc.vector.tensor_copy(x_picked[1][:], x_word_table[:].indirect(offs_list[:, 16:32]))
+        for c in range(2):
+            entries = offs_list[:, c * HALF_LIST : (c + 1) * HALF_LIST]
+            nc.vector.tensor_copy(x_picked[c][:], x_word_table[:].indirect(entries))
 
         w_bf = keep.tile([P, PACK, P, PACK], BF16, name="w_bf", align_bytes=64)
         for t in range(PACK):
             for c in range(2):
                 nc.scalar.copy(
-                    w_bf[:, t, c * 64 : (c + 1) * 64, :].rearrange("p (a i) j -> p a i j", i=4),
-                    w_raw[c].rearrange("p j (a t i) -> p t a i j", t=PACK, i=4)[:, t],
+                    w_bf[:, t, c * P // 2 : (c + 1) * P // 2, :].rearrange("p (a b) j -> p a b j", b=LINE_WORDS),
+                    w_raw[c].rearrange("p j (a t b) -> p t a b j", t=PACK, b=LINE_WORDS)[:, t],
                 )
         w_codes = keep.tile([P, N], U32, name="w_codes", align_bytes=64)
         w_scale = keep.tile([P, N], U8, name="w_scale", align_bytes=64)
@@ -113,13 +123,13 @@ def tile_picked_hpqihaarh_none_p_kernel(
 
         def first_product(c):
             bank = psum.tile([P, PACK, CHUNK], F32, name=f"h{c}", tag=f"bank{c}")
-            xs = x_picked[c // 2][:, (c % 2) * CHUNK : (c % 2 + 1) * CHUNK]
+            x_chunk = x_picked[c // 2][:, (c % 2) * CHUNK : (c % 2 + 1) * CHUNK]
             for t in range(PACK):
                 nc.tensor.matmul_mx(
                     bank[:, t, :],
                     lhsT=d_dealt[:, t * P : (t + 1) * P].bitcast(FP8X4),
                     lhsT_scale=planes[:, t * P : (t + 1) * P],
-                    rhs=xs.bitcast(FP8X4),
+                    rhs=x_chunk.bitcast(FP8X4),
                     rhs_scale=planes[:, H + c * CHUNK : H + (c + 1) * CHUNK],
                     start=True,
                     stop=True,
@@ -140,14 +150,14 @@ def tile_picked_hpqihaarh_none_p_kernel(
             )
 
         first_product(0)
-        for c in range(1, 4):
+        for c in range(1, PACK):
             first_product(c)
             quantize_z(c - 1)
         quantize_w(0, 1)
-        quantize_z(3)
+        quantize_z(PACK - 1)
         quantize_w(1, PACK)
 
-        def second_product(dst, t, cols):
+        def multiply_w(dst, t, cols):
             nc.tensor.matmul_mx(
                 dst,
                 lhsT=w_codes[:, t * P : (t + 1) * P].bitcast(FP8X4),
@@ -158,62 +168,79 @@ def tile_picked_hpqihaarh_none_p_kernel(
                 stop=True,
             )
 
-        out_rows = out.rearrange("(a t i) j -> t a i j", t=PACK, i=4)
-        h2, pa, pb, npb, dt = {}, {}, {}, {}, {}
+        out_rows = out.rearrange("(a t b) j -> t a b j", t=PACK, b=LINE_WORDS)
+        h2, pa, pb, minus_pb, dt, partners = {}, {}, {}, {}, {}, {}
 
-        def results(t):
+        def second_product(t):
             h2[t] = keep.tile([P, S], F32, name=f"h2_{t}", tag=f"row{t}")
             if t == 0:
                 early = psum.tile([P, S - CHUNK], F32, name="h2_early", tag="bank4")
                 late = psum.tile([P, CHUNK], F32, name="h2_late", tag="bank5")
-                second_product(early[:, 0:HALF], t, slice(0, HALF))
-                second_product(early[:, HALF : S - CHUNK], t, slice(HALF, S - CHUNK))
-                second_product(late[:], t, slice(S - CHUNK, S))
+                multiply_w(early[:, 0:HALF], t, slice(0, HALF))
+                multiply_w(early[:, HALF : S - CHUNK], t, slice(HALF, S - CHUNK))
+                multiply_w(late[:], t, slice(S - CHUNK, S))
                 nc.scalar.copy(h2[t][:, 0 : S - CHUNK], early[:])
                 nc.vector.tensor_copy(h2[t][:, S - CHUNK : S], late[:])
             else:
                 bank = psum.tile([P, S], F32, name=f"h2_bank{t}", tag=f"bank{(5 + t) % 8}")
-                second_product(bank[:], t, slice(0, S))
+                multiply_w(bank[:], t, slice(0, S))
                 nc.scalar.copy(h2[t][:], bank[:])
+
+        def gather_pairs(t):
             pa[t] = keep.tile([P, W], F32, name=f"pa{t}")
             pb[t] = keep.tile([P, W], F32, name=f"pb{t}")
-            npb[t] = keep.tile([P, W], F32, name=f"npb{t}")
+            minus_pb[t] = keep.tile([P, W], F32, name=f"minus_pb{t}")
             nc.scalar.activation(pa[t][:], h2[t][:].indirect(n1_list[:]), COPY)
             if t == 0:
                 nc.vector.tensor_copy(pb[t][:], h2[t][:].indirect(n2_list[:]))
             else:
                 nc.scalar.activation(pb[t][:], h2[t][:].indirect(n2_list[:]), COPY)
-            nc.scalar.activation(npb[t][:], pb[t][:], COPY, scale=-1.0)
+
+        def negate(t):
+            nc.scalar.activation(minus_pb[t][:], pb[t][:], COPY, scale=-1.0)
 
         def scatter_sums(t):
             dt[t] = keep.tile([P, S], F32, name=f"dt{t}")
             nc.vector.tensor_tensor(dt[t][:].indirect(n1_list[:]), pa[t][:], pb[t][:], ALU.add)
 
         def scatter_differences(t):
-            nc.vector.tensor_tensor(dt[t][:].indirect(n2_list[:]), pa[t][:], npb[t][:], ALU.add)
+            nc.vector.tensor_tensor(dt[t][:].indirect(n2_list[:]), pa[t][:], minus_pb[t][:], ALU.add)
+
+        def partner_buffer(t):
+            if t == 0:
+                partners[0] = keep.tile([P, S], F32, name="partner0", tag="row2")[:]
+            elif t == 1:
+                both = keep.tile([P, 2 * S], F32, name="partners12", tag="row3")
+                partners[1], partners[2] = both[:, 0:S], both[:, S : 2 * S]
+            elif t == 3:
+                partners[3] = keep.tile([P, S], F32, name="partner3", tag="row0")[:]
+            return partners[t]
 
         def larger(t):
-            partner = keep.tile([P, S], F32, name=f"partner{t}", tag=f"row{(t + 1) % PACK}")
+            partner = partner_buffer(t)
             result = keep.tile([P, S], F32, name=f"result{t}")
-            last = t == PACK - 1
             halves = [slice(c * HALF, (c + 1) * HALF) for c in range(2)]
-            nc.scalar.activation(partner[:, halves[0]], dt[t][:].indirect(n3_list[:, 0:16]), COPY)
-            if last:
-                nc.vector.tensor_copy(partner[:, halves[1]], dt[t][:].indirect(n3_list[:, 16:32]))
-                for cols in reversed(halves):
+            windows = [dt[t][:].indirect(n3_list[:, c * HALF_LIST : (c + 1) * HALF_LIST]) for c in range(2)]
+            nc.scalar.activation(partner[:, halves[0]], windows[0], COPY)
+            if t == PACK - 1:
+                nc.vector.tensor_copy(partner[:, halves[1]], windows[1])
+                for cols, queue in zip(halves, (nc.sync, nc.scalar)):
                     nc.vector.tensor_tensor(result[:, cols], dt[t][:, cols], partner[:, cols], ALU.max)
-                    nc.sync.dma_start(out_rows[t][:, :, cols], result[:, cols])
+                    queue.dma_start(out_rows[t][:, :, cols], result[:, cols])
             else:
-                nc.scalar.activation(partner[:, halves[1]], dt[t][:].indirect(n3_list[:, 16:32]), COPY)
-                nc.vector.tensor_tensor(result[:], dt[t][:], partner[:], ALU.max)
+                nc.scalar.activation(partner[:, halves[1]], windows[1], COPY)
+                nc.vector.tensor_tensor(result[:], dt[t][:], partner, ALU.max)
                 nc.sync.dma_start(out_rows[t], result[:])
 
-        results(0)
-        scatter_sums(0)
-        scatter_differences(0)
-        for t in range(1, PACK):
-            results(t)
+        second_product(0)
+        for t in range(PACK):
+            gather_pairs(t)
             scatter_sums(t)
-            larger(t - 1)
+            if t + 1 < PACK:
+                second_product(t + 1)
+            if t >= LAG:
+                larger(t - LAG)
+            negate(t)
             scatter_differences(t)
-        larger(PACK - 1)
+        for t in range(PACK - LAG, PACK):
+            larger(t)

from contextlib import ExitStack

import concourse.mybir as mybir

K, T, S, H, N, W = 512, 2048, 512, 512, 512, 256
FLOPS = 2 * K * H * S + 2 * H * N * S

F32 = mybir.dt.float32
BF16 = mybir.dt.bfloat16
I32 = mybir.dt.int32
U32 = mybir.dt.uint32
U16 = mybir.dt.uint16
U8 = mybir.dt.uint8
FP8X4 = mybir.dt.float8_e4m3fn_x4
ALU = mybir.AluOpType
COPY = mybir.ActivationFunctionType.Copy

P = 128
PACK = 4
BLOCK_ROWS = 8
QUADRANT = 32
CHUNK = S // PACK
HALF = S // 2
HALF_LIST = HALF // 16
LINE_WORDS = 4
LINE_BYTES = 16
LAG = 2


def tile_picked_hpqihaarh_none_p_kernel(
    tc, x_words, x_scales, d_words, d_scales, gn, w1, offs, k1, n1, n2, n3, out
):
    nc = tc.nc
    with ExitStack() as ctx:
        keep = ctx.enter_context(tc.tile_pool(name="keep", bufs=1))
        psum = ctx.enter_context(tc.psum_pool(name="psum", bufs=1))

        def load_list(name, lists):
            tile = keep.tile(list(lists.shape), U16, name=name)
            nc.sync.dma_start(tile[:], lists)
            return tile

        def load_scales(name, scales, clearing_engine):
            tile = keep.tile([P, T], U8, name=name, align_bytes=64)
            clearing_engine.memset(tile[:].bitcast(I32), 0)
            nc.sync.dma_start(tile[0:P:BLOCK_ROWS, :].bitcast(I32), scales[0].bitcast(I32))
            return tile

        def load_words(name, words):
            tile = keep.tile([P, T], U32, name=name, align_bytes=64)
            nc.sync.dma_start(tile[:].bitcast(I32), words[0].rearrange("p n t -> p (n t)").bitcast(I32))
            return tile

        d_scale_table = load_scales("d_scale_table", d_scales, nc.gpsimd)
        x_scale_table = load_scales("x_scale_table", x_scales, nc.vector)
        k1_list = load_list("k1_list", k1)
        offs_list = load_list("offs_list", offs)
        n1_list = load_list("n1_list", n1)
        n2_list = load_list("n2_list", n2)
        n3_list = load_list("n3_list", n3)
        d_word_table = load_words("d_word_table", d_words)
        gain = keep.tile([P, PACK], F32, name="gain")
        nc.sync.dma_start(gain[:], gn.rearrange("(p t) o -> p (t o)", t=PACK))
        x_word_table = load_words("x_word_table", x_words)

        gain16 = keep.tile([P, PACK], F32, name="gain16")
        nc.scalar.activation(gain16[:], gain[:], COPY, scale=0.0625)

        d_scale_picked = keep.tile([P, H], U8, name="d_scale_picked", align_bytes=64)
        x_scale_picked = keep.tile([P, S], U8, name="x_scale_picked", tag="stage", align_bytes=64)
        planes = keep.tile([P, H + S], U8, name="planes", align_bytes=64)
        nc.vector.tensor_copy(d_scale_picked[:], d_scale_table[:].indirect(k1_list[:]))
        nc.vector.tensor_copy(x_scale_picked[:], x_scale_table[:].indirect(offs_list[:]))
        nc.vector.tensor_copy(
            planes[:, 0:H].rearrange("p (t a b) -> p a t b", t=PACK, b=LINE_BYTES),
            d_scale_picked[:].rearrange("p (a b t) -> p a t b", t=PACK, b=LINE_BYTES),
        )
        nc.vector.tensor_copy(planes[:, H : H + S].bitcast(I32), x_scale_picked[:].bitcast(I32))
        for a in range(1, PACK):
            nc.sync.dma_start(
                planes[a:P:QUADRANT, :].bitcast(I32), planes[BLOCK_ROWS * a : P : QUADRANT, :].bitcast(I32)
            )

        w_rows = w1.rearrange("(p j) c -> p j c", j=PACK)
        w_tile = keep.tile([P, PACK * N], F32, name="w_tile", tag="stage", align_bytes=64)
        w_raw = []
        for c in range(2):
            piece = w_tile[:, c * PACK * HALF : (c + 1) * PACK * HALF].rearrange("p (j c) -> p j c", j=PACK)
            nc.sync.dma_start(piece, w_rows[:, :, c * HALF : (c + 1) * HALF])
            w_raw.append(piece)

        d_picked = keep.tile([P, H], U32, name="d_picked", align_bytes=64)
        d_dealt = keep.tile([P, H], U32, name="d_dealt", align_bytes=64)
        nc.vector.tensor_copy(d_picked[:], d_word_table[:].indirect(k1_list[:]))
        x_picked = [keep.tile([P, HALF], U32, name=f"x_picked{c}", align_bytes=64) for c in range(2)]
        nc.vector.tensor_copy(
            d_dealt[:].rearrange("p (t a b) -> p a t b", t=PACK, b=LINE_WORDS),
            d_picked[:].rearrange("p (a b t) -> p a t b", t=PACK, b=LINE_WORDS),
        )
        for c in range(2):
            entries = offs_list[:, c * HALF_LIST : (c + 1) * HALF_LIST]
            nc.vector.tensor_copy(x_picked[c][:], x_word_table[:].indirect(entries))

        w_bf = keep.tile([P, PACK, P, PACK], BF16, name="w_bf", align_bytes=64)
        for t in range(PACK):
            for c in range(2):
                nc.scalar.copy(
                    w_bf[:, t, c * P // 2 : (c + 1) * P // 2, :].rearrange("p (a b) j -> p a b j", b=LINE_WORDS),
                    w_raw[c].rearrange("p j (a t b) -> p t a b j", t=PACK, b=LINE_WORDS)[:, t],
                )
        w_codes = keep.tile([P, N], U32, name="w_codes", align_bytes=64)
        w_scale = keep.tile([P, N], U8, name="w_scale", align_bytes=64)

        def quantize_w(t0, t1):
            cols = slice(t0 * P, t1 * P)
            nc.vector.quantize_mx(
                w_codes[:, cols].bitcast(FP8X4), w_scale[:, cols], w_bf[:, t0:t1].rearrange("p t m j -> p (t m j)")
            )

        z_codes = keep.tile([P, S], U32, name="z_codes", align_bytes=64)
        z_scale = keep.tile([P, S], U8, name="z_scale", align_bytes=64)
        z_bf = []

        def first_product(c):
            bank = psum.tile([P, PACK, CHUNK], F32, name=f"h{c}", tag=f"bank{c}")
            x_chunk = x_picked[c // 2][:, (c % 2) * CHUNK : (c % 2 + 1) * CHUNK]
            for t in range(PACK):
                nc.tensor.matmul_mx(
                    bank[:, t, :],
                    lhsT=d_dealt[:, t * P : (t + 1) * P].bitcast(FP8X4),
                    lhsT_scale=planes[:, t * P : (t + 1) * P],
                    rhs=x_chunk.bitcast(FP8X4),
                    rhs_scale=planes[:, H + c * CHUNK : H + (c + 1) * CHUNK],
                    start=True,
                    stop=True,
                )
            z = keep.tile([P, CHUNK, PACK], BF16, name=f"z_bf{c}", align_bytes=64)
            nc.vector.tensor_tensor(
                z[:],
                bank[:].rearrange("p t n -> p n t"),
                gain16[:].unsqueeze(1).to_broadcast([P, CHUNK, PACK]),
                ALU.mult,
            )
            z_bf.append(z)

        def quantize_z(c):
            cols = slice(c * CHUNK, (c + 1) * CHUNK)
            nc.vector.quantize_mx(
                z_codes[:, cols].bitcast(FP8X4), z_scale[:, cols], z_bf[c][:].rearrange("p n t -> p (n t)")
            )

        first_product(0)
        for c in range(1, PACK):
            first_product(c)
            quantize_z(c - 1)
        quantize_w(0, 1)
        quantize_z(PACK - 1)
        quantize_w(1, PACK)

        def multiply_w(dst, t, cols):
            nc.tensor.matmul_mx(
                dst,
                lhsT=w_codes[:, t * P : (t + 1) * P].bitcast(FP8X4),
                lhsT_scale=w_scale[:, t * P : (t + 1) * P],
                rhs=z_codes[:, cols].bitcast(FP8X4),
                rhs_scale=z_scale[:, cols],
                start=True,
                stop=True,
            )

        out_rows = out.rearrange("(a t b) j -> t a b j", t=PACK, b=LINE_WORDS)
        h2, pa, pb, minus_pb, dt, partners = {}, {}, {}, {}, {}, {}

        def second_product(t):
            h2[t] = keep.tile([P, S], F32, name=f"h2_{t}", tag=f"row{t}")
            if t == 0:
                early = psum.tile([P, S - CHUNK], F32, name="h2_early", tag="bank4")
                late = psum.tile([P, CHUNK], F32, name="h2_late", tag="bank5")
                multiply_w(early[:, 0:HALF], t, slice(0, HALF))
                multiply_w(early[:, HALF : S - CHUNK], t, slice(HALF, S - CHUNK))
                multiply_w(late[:], t, slice(S - CHUNK, S))
                nc.scalar.copy(h2[t][:, 0 : S - CHUNK], early[:])
                nc.vector.tensor_copy(h2[t][:, S - CHUNK : S], late[:])
            else:
                bank = psum.tile([P, S], F32, name=f"h2_bank{t}", tag=f"bank{(5 + t) % 8}")
                multiply_w(bank[:], t, slice(0, S))
                nc.scalar.copy(h2[t][:], bank[:])

        def gather_pairs(t):
            pa[t] = keep.tile([P, W], F32, name=f"pa{t}")
            pb[t] = keep.tile([P, W], F32, name=f"pb{t}")
            minus_pb[t] = keep.tile([P, W], F32, name=f"minus_pb{t}")
            nc.scalar.activation(pa[t][:], h2[t][:].indirect(n1_list[:]), COPY)
            if t == 0:
                nc.vector.tensor_copy(pb[t][:], h2[t][:].indirect(n2_list[:]))
            else:
                nc.scalar.activation(pb[t][:], h2[t][:].indirect(n2_list[:]), COPY)

        def negate(t):
            nc.scalar.activation(minus_pb[t][:], pb[t][:], COPY, scale=-1.0)

        def scatter_sums(t):
            dt[t] = keep.tile([P, S], F32, name=f"dt{t}")
            nc.vector.tensor_tensor(dt[t][:].indirect(n1_list[:]), pa[t][:], pb[t][:], ALU.add)

        def scatter_differences(t):
            nc.vector.tensor_tensor(dt[t][:].indirect(n2_list[:]), pa[t][:], minus_pb[t][:], ALU.add)

        def partner_buffer(t):
            if t == 0:
                partners[0] = keep.tile([P, S], F32, name="partner0", tag="row2")[:]
            elif t == 1:
                both = keep.tile([P, 2 * S], F32, name="partners12", tag="row3")
                partners[1], partners[2] = both[:, 0:S], both[:, S : 2 * S]
            elif t == 3:
                partners[3] = keep.tile([P, S], F32, name="partner3", tag="row0")[:]
            return partners[t]

        def larger(t):
            partner = partner_buffer(t)
            result = keep.tile([P, S], F32, name=f"result{t}")
            halves = [slice(c * HALF, (c + 1) * HALF) for c in range(2)]
            windows = [dt[t][:].indirect(n3_list[:, c * HALF_LIST : (c + 1) * HALF_LIST]) for c in range(2)]
            nc.scalar.activation(partner[:, halves[0]], windows[0], COPY)
            if t == PACK - 1:
                nc.vector.tensor_copy(partner[:, halves[1]], windows[1])
                for cols, queue in zip(halves, (nc.sync, nc.scalar)):
                    nc.vector.tensor_tensor(result[:, cols], dt[t][:, cols], partner[:, cols], ALU.max)
                    queue.dma_start(out_rows[t][:, :, cols], result[:, cols])
            else:
                nc.scalar.activation(partner[:, halves[1]], windows[1], COPY)
                nc.vector.tensor_tensor(result[:], dt[t][:], partner, ALU.max)
                nc.sync.dma_start(out_rows[t], result[:])

        second_product(0)
        for t in range(PACK):
            gather_pairs(t)
            scatter_sums(t)
            if t + 1 < PACK:
                second_product(t + 1)
            if t >= LAG:
                larger(t - LAG)
            negate(t)
            scatter_differences(t)
        for t in range(PACK - LAG, PACK):
            larger(t)
